import numpy as np
import ml_dtypes


def mxq(x, axis, fmt="e4m3"):
    dtype, down = {"e4m3": (ml_dtypes.float8_e4m3fn, 7), "e5m2": (ml_dtypes.float8_e5m2, 14)}[fmt]
    v = np.moveaxis(np.asarray(x, np.float32).astype(ml_dtypes.bfloat16).astype(np.float64), axis, -1)
    blocks = v.reshape(v.shape[:-1] + (-1, 32))
    amax = np.abs(blocks).max(-1, keepdims=True)
    byte = np.maximum(np.where(amax > 0, np.frexp(amax)[1] - 1 + 127, 0) - down, 1)
    scale = np.exp2(byte - 127.0)
    codes = (blocks / scale).astype(np.float32).astype(dtype).astype(np.float64)
    return np.moveaxis((codes * scale).reshape(v.shape), -1, axis)


WIDE = False


def mx_kscale(k):
    if not WIDE:
        return np.ones(k)
    levels = np.array([30, -30])
    if k % 512:
        return np.exp2(np.random.permutation(np.resize(levels, k // 32))).repeat(32)
    a = np.empty((k // 512, 16))
    for p in range(k // 512):
        a[p, :8] = np.random.permutation(np.resize(levels, 8))
        for g in range(8):
            far = levels[np.abs(levels - a[p, g]) >= 10]
            a[p, g + 8] = far[np.random.randint(len(far))]
    return np.exp2(a.ravel()).repeat(32)


def f64(x):
    return np.asarray(x).astype(np.float64)


def striped(idx):
    return np.tile(np.asarray(idx).reshape(-1, 16).T, (8, 1)).astype(np.uint16)


def unstriped(offs):
    return offs[:16].T.reshape(-1).astype(np.int64)


K, T, J, N, I = 512, 2048, 512, 2048, 512


def setup_inputs():
    n = np.random.standard_normal
    idx = np.random.permutation(T)[:J]
    idx2 = np.random.permutation(N)[:I]
    fj = mx_kscale(J)
    tj = np.ones(T)
    tj[idx] = fj
    return {
        "xt": (n((K, T)) * tj).astype(np.float32),
        "gj": (n((J, N)) * np.exp(0.5 * n((J, 1))) / fj[:, None]).astype(np.float32),
        "mom": (1.0 * n((K, N))).astype(np.float32),
        "offs": striped(idx),
        "offs2": striped(idx2),
    }


def reference(xt, gj, mom, offs, offs2):
    idx = unstriped(offs)
    idx2 = unstriped(offs2)
    xj = f64(xt)[:, idx].T
    xjq = mxq(xj, 0, "e4m3")
    gjidx2q = mxq(f64(gj)[:, idx2], 0, "e5m2")
    w = xjq.T @ gjidx2q
    d = 0.04 * w + 0.9 * f64(mom)[:, idx2]
    y = np.tanh(d)
    return y

@@ -1,0 +1,117 @@
+from contextlib import ExitStack
+
+import concourse.mybir as mybir
+from concourse.masks import make_identity
+
+K, T, J, N, I = 512, 2048, 512, 2048, 512
+FLOPS = 2 * K * J * I
+
+F32 = mybir.dt.float32
+BF16 = mybir.dt.bfloat16
+U32 = mybir.dt.uint32
+U16 = mybir.dt.uint16
+U8 = mybir.dt.uint8
+E4M3X4 = mybir.dt.float8_e4m3fn_x4
+E5M2X4 = mybir.dt.float8_e5m2_x4
+ACT = mybir.ActivationFunctionType
+ALU = mybir.AluOpType
+
+P = 128
+PACK = 4
+GRAD_SCALE = 0.04
+MOM_SCALE = 0.9
+LAST_PIECES = (256, 128, 128)
+
+
+def tile_list_wgrad_lists_on_both_sides_kernel(tc, xt, gj, mom, offs, offs2, out):
+    nc = tc.nc
+    xt_rows = xt.rearrange("(p t) n -> p t n", t=PACK)
+    gj_rows = gj.rearrange("(p t) n -> p t n", t=PACK)
+    mom_rows = mom.rearrange("(p t) n -> p t n", t=PACK)
+    out_rows = out.rearrange("(p t) n -> p t n", t=PACK)
+
+    with ExitStack() as ctx:
+        keep = ctx.enter_context(tc.tile_pool(name="keep", bufs=1))
+        stage = ctx.enter_context(tc.tile_pool(name="stage", bufs=2))
+        psum = ctx.enter_context(tc.psum_pool(name="psum", bufs=2))
+
+        tok = keep.tile([P, J // 16], U16, name="tok")
+        feat = keep.tile([P, I // 16], U16, name="feat")
+        g_win = [keep.tile([P, N], F32, name="g_win%d" % t) for t in range(PACK)]
+        x_win = [keep.tile([P, T], F32, name="x_win%d" % t) for t in range(PACK)]
+        m_win = [keep.tile([P, N], F32, name="m_win%d" % t) for t in range(PACK)]
+
+        nc.sync.dma_start(g_win[0][:], gj_rows[:, 0, :])
+        nc.sync.dma_start(feat[:], offs2)
+        nc.sync.dma_start(tok[:], offs)
+        for t in range(1, PACK):
+            nc.sync.dma_start(g_win[t][:], gj_rows[:, t, :])
+        for t in range(PACK):
+            nc.sync.dma_start(x_win[t][:], xt_rows[:, t, :])
+        for t in range(PACK):
+            nc.sync.dma_start(m_win[t][:], mom_rows[:, t, :])
+
+        ident = keep.tile([P, P], F32, name="ident")
+        make_identity(nc, ident[:])
+
+        g_grouped = keep.tile([P, I, PACK], BF16, name="g_grouped", align_bytes=64)
+        for t in range(PACK):
+            nc.vector.tensor_copy(g_grouped[:, :, t], g_win[t][:].indirect(feat[:]))
+        g_codes = keep.tile([P, I], U32, name="g_codes", align_bytes=64)
+        g_scales = keep.tile([P, I], U8, name="g_scales", align_bytes=64)
+        nc.vector.quantize_mx(
+            out=g_codes[:].bitcast(E5M2X4),
+            scales=g_scales[:],
+            in_=g_grouped[:].rearrange("p i t -> p (i t)"),
+        )
+
+        w_scaled = [keep.tile([P, I], F32, name="w_scaled%d" % t) for t in range(PACK)]
+        for t in range(PACK):
+            x_picked = stage.tile([P, J], BF16, name="x_picked")
+            nc.scalar.activation(x_picked[:], x_win[t][:].indirect(tok[:]), ACT.Copy)
+            words = x_picked[:].bitcast(F32)
+            turned = psum.tile([P, 2, P], F32, name="turned")
+            for u in range(2):
+                nc.tensor.transpose(turned[:, u, :], words[:, u : J // 2 : 2], ident[:])
+            x_grouped = stage.tile([P, P * PACK], BF16, name="x_grouped", align_bytes=64)
+            nc.vector.tensor_copy(
+                x_grouped[:].bitcast(F32).rearrange("p (r u) -> p r u", u=2),
+                turned[:].rearrange("p u r -> p r u"),
+            )
+            x_codes = stage.tile([P, P], U32, name="x_codes", align_bytes=64)
+            x_scales = stage.tile([P, P], U8, name="x_scales", align_bytes=64)
+            nc.vector.quantize_mx(out=x_codes[:].bitcast(E4M3X4), scales=x_scales[:], in_=x_grouped[:])
+            w = psum.tile([P, I], F32, name="w")
+            nc.tensor.matmul_mx(
+                out=w[:],
+                lhsT=x_codes[:].bitcast(E4M3X4),
+                lhsT_scale=x_scales[:],
+                rhs=g_codes[:].bitcast(E5M2X4),
+                rhs_scale=g_scales[:],
+                start=True,
+                stop=True,
+            )
+            nc.scalar.activation(w_scaled[t][:], w[:], ACT.Copy, scale=GRAD_SCALE / MOM_SCALE)
+
+        early = keep.tile([P, PACK - 1, I], F32, name="early")
+        for t in range(PACK - 1):
+            mixed = stage.tile([P, I], F32, name="mixed")
+            nc.vector.tensor_tensor(mixed[:], m_win[t][:].indirect(feat[:]), w_scaled[t][:], ALU.add)
+            nc.scalar.activation(early[:, t, :], mixed[:], ACT.Tanh, scale=MOM_SCALE)
+        nc.sync.dma_start(out_rows[:, 0 : PACK - 1, :], early[:])
+
+        t = PACK - 1
+        c0 = 0
+        for n, width in enumerate(LAST_PIECES):
+            cols = slice(c0, c0 + width)
+            mixed_piece = keep.tile([P, width], F32, name="mixed_piece%d" % n)
+            nc.vector.tensor_tensor(
+                mixed_piece[:],
+                m_win[t][:].indirect(feat[:, c0 // 16 : (c0 + width) // 16]),
+                w_scaled[t][:, cols],
+                ALU.add,
+            )
+            late = keep.tile([P, width], F32, name="late%d" % n)
+            nc.scalar.activation(late[:], mixed_piece[:], ACT.Tanh, scale=MOM_SCALE)
+            nc.sync.dma_start(out_rows[:, t, cols], late[:])
+            c0 = c0 + width

@@ -20,7 +20,7 @@ P = 128
 PACK = 4
 GRAD_SCALE = 0.04
 MOM_SCALE = 0.9
-LAST_PIECES = (256, 128, 128)
+FUSED = 256
 
 
 def tile_list_wgrad_lists_on_both_sides_kernel(tc, xt, gj, mom, offs, offs2, out):
@@ -34,6 +34,7 @@ def tile_list_wgrad_lists_on_both_sides_kernel(tc, xt, gj, mom, offs, offs2, out
         keep = ctx.enter_context(tc.tile_pool(name="keep", bufs=1))
         stage = ctx.enter_context(tc.tile_pool(name="stage", bufs=2))
         psum = ctx.enter_context(tc.psum_pool(name="psum", bufs=2))
+        banks = ctx.enter_context(tc.psum_pool(name="banks", bufs=1))
 
         tok = keep.tile([P, J // 16], U16, name="tok")
         feat = keep.tile([P, I // 16], U16, name="feat")
@@ -65,7 +66,7 @@ def tile_list_wgrad_lists_on_both_sides_kernel(tc, xt, gj, mom, offs, offs2, out
             in_=g_grouped[:].rearrange("p i t -> p (i t)"),
         )
 
-        w_scaled = [keep.tile([P, I], F32, name="w_scaled%d" % t) for t in range(PACK)]
+        sums = []
         for t in range(PACK):
             x_picked = stage.tile([P, J], BF16, name="x_picked")
             nc.scalar.activation(x_picked[:], x_win[t][:].indirect(tok[:]), ACT.Copy)
@@ -81,7 +82,7 @@ def tile_list_wgrad_lists_on_both_sides_kernel(tc, xt, gj, mom, offs, offs2, out
             x_codes = stage.tile([P, P], U32, name="x_codes", align_bytes=64)
             x_scales = stage.tile([P, P], U8, name="x_scales", align_bytes=64)
             nc.vector.quantize_mx(out=x_codes[:].bitcast(E4M3X4), scales=x_scales[:], in_=x_grouped[:])
-            w = psum.tile([P, I], F32, name="w")
+            w = banks.tile([P, I], F32, name="w%d" % t)
             nc.tensor.matmul_mx(
                 out=w[:],
                 lhsT=x_codes[:].bitcast(E4M3X4),
@@ -91,27 +92,36 @@ def tile_list_wgrad_lists_on_both_sides_kernel(tc, xt, gj, mom, offs, offs2, out
                 start=True,
                 stop=True,
             )
-            nc.scalar.activation(w_scaled[t][:], w[:], ACT.Copy, scale=GRAD_SCALE / MOM_SCALE)
+            sums.append(w)
 
-        early = keep.tile([P, PACK - 1, I], F32, name="early")
-        for t in range(PACK - 1):
+        last = PACK - 1
+        fused = slice(0, FUSED)
+        plain = slice(FUSED, I)
+        w_last = keep.tile([P, FUSED], F32, name="w_last")
+        nc.scalar.activation(w_last[:], sums[last][:, fused], ACT.Copy, scale=GRAD_SCALE / MOM_SCALE)
+
+        for t in range(last):
+            m_picked = stage.tile([P, I], F32, name="m_picked")
+            nc.vector.tensor_copy(m_picked[:], m_win[t][:].indirect(feat[:]))
             mixed = stage.tile([P, I], F32, name="mixed")
-            nc.vector.tensor_tensor(mixed[:], m_win[t][:].indirect(feat[:]), w_scaled[t][:], ALU.add)
-            nc.scalar.activation(early[:, t, :], mixed[:], ACT.Tanh, scale=MOM_SCALE)
-        nc.sync.dma_start(out_rows[:, 0 : PACK - 1, :], early[:])
-
-        t = PACK - 1
-        c0 = 0
-        for n, width in enumerate(LAST_PIECES):
-            cols = slice(c0, c0 + width)
-            mixed_piece = keep.tile([P, width], F32, name="mixed_piece%d" % n)
-            nc.vector.tensor_tensor(
-                mixed_piece[:],
-                m_win[t][:].indirect(feat[:, c0 // 16 : (c0 + width) // 16]),
-                w_scaled[t][:, cols],
-                ALU.add,
+            nc.vector.scalar_tensor_tensor(
+                mixed[:], sums[t][:], GRAD_SCALE / MOM_SCALE, m_picked[:], ALU.mult, ALU.add
             )
-            late = keep.tile([P, width], F32, name="late%d" % n)
-            nc.scalar.activation(late[:], mixed_piece[:], ACT.Tanh, scale=MOM_SCALE)
-            nc.sync.dma_start(out_rows[:, t, cols], late[:])
-            c0 = c0 + width
+            result = keep.tile([P, I], F32, name="result%d" % t)
+            nc.scalar.activation(result[:], mixed[:], ACT.Tanh, scale=MOM_SCALE)
+            nc.sync.dma_start(out_rows[:, t, :], result[:])
+
+        mixed_a = keep.tile([P, FUSED], F32, name="mixed_a")
+        nc.vector.tensor_tensor(mixed_a[:], m_win[last][:].indirect(feat[:, 0 : FUSED // 16]), w_last[:], ALU.add)
+        picked_b = keep.tile([P, I - FUSED], F32, name="picked_b")
+        nc.scalar.activation(picked_b[:], m_win[last][:].indirect(feat[:, FUSED // 16 : I // 16]), ACT.Copy)
+        mixed_b = keep.tile([P, I - FUSED], F32, name="mixed_b")
+        nc.vector.scalar_tensor_tensor(
+            mixed_b[:], sums[last][:, plain], GRAD_SCALE / MOM_SCALE, picked_b[:], ALU.mult, ALU.add
+        )
+        result_a = keep.tile([P, FUSED], F32, name="result_a")
+        nc.scalar.activation(result_a[:], mixed_a[:], ACT.Tanh, scale=MOM_SCALE)
+        nc.sync.dma_start(out_rows[:, last, fused], result_a[:])
+        result_b = keep.tile([P, I - FUSED], F32, name="result_b")
+        nc.scalar.activation(result_b[:], mixed_b[:], ACT.Tanh, scale=MOM_SCALE)
+        nc.sync.dma_start(out_rows[:, last, plain], result_b[:])

@@ -21,6 +21,7 @@ PACK = 4
 GRAD_SCALE = 0.04
 MOM_SCALE = 0.9
 FUSED = 256
+PIECE = 128
 
 
 def tile_list_wgrad_lists_on_both_sides_kernel(tc, xt, gj, mom, offs, offs2, out):
@@ -38,8 +39,8 @@ def tile_list_wgrad_lists_on_both_sides_kernel(tc, xt, gj, mom, offs, offs2, out
 
         tok = keep.tile([P, J // 16], U16, name="tok")
         feat = keep.tile([P, I // 16], U16, name="feat")
-        g_win = [keep.tile([P, N], F32, name="g_win%d" % t) for t in range(PACK)]
         x_win = [keep.tile([P, T], F32, name="x_win%d" % t) for t in range(PACK)]
+        g_win = [keep.tile([P, N], F32, name="g_win%d" % t) for t in range(PACK)]
         m_win = [keep.tile([P, N], F32, name="m_win%d" % t) for t in range(PACK)]
 
         nc.sync.dma_start(g_win[0][:], gj_rows[:, 0, :])
@@ -55,9 +56,14 @@ def tile_list_wgrad_lists_on_both_sides_kernel(tc, xt, gj, mom, offs, offs2, out
         ident = keep.tile([P, P], F32, name="ident")
         make_identity(nc, ident[:])
 
-        g_grouped = keep.tile([P, I, PACK], BF16, name="g_grouped", align_bytes=64)
+        g_picked = keep.tile([P, PACK, I], BF16, name="g_picked")
         for t in range(PACK):
-            nc.vector.tensor_copy(g_grouped[:, :, t], g_win[t][:].indirect(feat[:]))
+            nc.scalar.activation(g_picked[:, t, :], g_win[t][:].indirect(feat[:]), ACT.Copy)
+        g_grouped = keep.tile([P, I, PACK], BF16, name="g_grouped", align_bytes=64)
+        nc.vector.tensor_copy(
+            g_grouped[:].rearrange("p (c i) t -> p c t i", i=4),
+            g_picked[:].rearrange("p t (c i) -> p c t i", i=4),
+        )
         g_codes = keep.tile([P, I], U32, name="g_codes", align_bytes=64)
         g_scales = keep.tile([P, I], U8, name="g_scales", align_bytes=64)
         nc.vector.quantize_mx(
@@ -66,7 +72,10 @@ def tile_list_wgrad_lists_on_both_sides_kernel(tc, xt, gj, mom, offs, offs2, out
             in_=g_grouped[:].rearrange("p i t -> p (i t)"),
         )
 
+        fused = slice(0, FUSED)
+        plain = slice(FUSED, I)
         sums = []
+        w_scaled = []
         for t in range(PACK):
             x_picked = stage.tile([P, J], BF16, name="x_picked")
             nc.scalar.activation(x_picked[:], x_win[t][:].indirect(tok[:]), ACT.Copy)
@@ -93,35 +102,40 @@ def tile_list_wgrad_lists_on_both_sides_kernel(tc, xt, gj, mom, offs, offs2, out
                 stop=True,
             )
             sums.append(w)
+            scaled = stage.tile([P, FUSED], F32, name="scaled")
+            nc.vector.tensor_scalar(scaled[:], w[:, fused], GRAD_SCALE / MOM_SCALE, None, ALU.mult)
+            w_scaled.append(scaled)
 
-        last = PACK - 1
-        fused = slice(0, FUSED)
-        plain = slice(FUSED, I)
-        w_last = keep.tile([P, FUSED], F32, name="w_last")
-        nc.scalar.activation(w_last[:], sums[last][:, fused], ACT.Copy, scale=GRAD_SCALE / MOM_SCALE)
-
-        for t in range(last):
-            m_picked = stage.tile([P, I], F32, name="m_picked")
-            nc.vector.tensor_copy(m_picked[:], m_win[t][:].indirect(feat[:]))
-            mixed = stage.tile([P, I], F32, name="mixed")
-            nc.vector.scalar_tensor_tensor(
-                mixed[:], sums[t][:], GRAD_SCALE / MOM_SCALE, m_picked[:], ALU.mult, ALU.add
-            )
+        for t in range(PACK):
             result = keep.tile([P, I], F32, name="result%d" % t)
-            nc.scalar.activation(result[:], mixed[:], ACT.Tanh, scale=MOM_SCALE)
-            nc.sync.dma_start(out_rows[:, t, :], result[:])
-
-        mixed_a = keep.tile([P, FUSED], F32, name="mixed_a")
-        nc.vector.tensor_tensor(mixed_a[:], m_win[last][:].indirect(feat[:, 0 : FUSED // 16]), w_last[:], ALU.add)
-        picked_b = keep.tile([P, I - FUSED], F32, name="picked_b")
-        nc.scalar.activation(picked_b[:], m_win[last][:].indirect(feat[:, FUSED // 16 : I // 16]), ACT.Copy)
-        mixed_b = keep.tile([P, I - FUSED], F32, name="mixed_b")
-        nc.vector.scalar_tensor_tensor(
-            mixed_b[:], sums[last][:, plain], GRAD_SCALE / MOM_SCALE, picked_b[:], ALU.mult, ALU.add
-        )
-        result_a = keep.tile([P, FUSED], F32, name="result_a")
-        nc.scalar.activation(result_a[:], mixed_a[:], ACT.Tanh, scale=MOM_SCALE)
-        nc.sync.dma_start(out_rows[:, last, fused], result_a[:])
-        result_b = keep.tile([P, I - FUSED], F32, name="result_b")
-        nc.scalar.activation(result_b[:], mixed_b[:], ACT.Tanh, scale=MOM_SCALE)
-        nc.sync.dma_start(out_rows[:, last, plain], result_b[:])
+            mixed = stage.tile([P, I], F32, name="mixed")
+            picked = stage.tile([P, I - FUSED], F32, name="picked")
+            for c in range(0, FUSED, PIECE):
+                nc.vector.tensor_tensor(
+                    mixed[:, c : c + PIECE],
+                    m_win[t][:].indirect(feat[:, c // 16 : (c + PIECE) // 16]),
+                    w_scaled[t][:, c : c + PIECE],
+                    ALU.add,
+                )
+            for c in range(FUSED, I, PIECE):
+                nc.scalar.activation(
+                    picked[:, c - FUSED : c - FUSED + PIECE],
+                    m_win[t][:].indirect(feat[:, c // 16 : (c + PIECE) // 16]),
+                    ACT.Copy,
+                )
+            for c in range(FUSED, I, PIECE):
+                nc.vector.scalar_tensor_tensor(
+                    mixed[:, c : c + PIECE],
+                    sums[t][:, c : c + PIECE],
+                    GRAD_SCALE / MOM_SCALE,
+                    picked[:, c - FUSED : c - FUSED + PIECE],
+                    ALU.mult,
+                    ALU.add,
+                )
+            for c in range(0, I, PIECE):
+                nc.scalar.activation(result[:, c : c + PIECE], mixed[:, c : c + PIECE], ACT.Tanh, scale=MOM_SCALE)
+            if t < PACK - 1:
+                nc.sync.dma_start(out_rows[:, t, :], result[:])
+            else:
+                nc.sync.dma_start(out_rows[:, t, fused], result[:, fused])
+                nc.scalar.dma_start(out_rows[:, t, plain], result[:, plain])

from contextlib import ExitStack

import concourse.mybir as mybir
from concourse.masks import make_identity

K, T, J, N, I = 512, 2048, 512, 2048, 512
FLOPS = 2 * K * J * I

F32 = mybir.dt.float32
BF16 = mybir.dt.bfloat16
U32 = mybir.dt.uint32
U16 = mybir.dt.uint16
U8 = mybir.dt.uint8
E4M3X4 = mybir.dt.float8_e4m3fn_x4
E5M2X4 = mybir.dt.float8_e5m2_x4
ACT = mybir.ActivationFunctionType
ALU = mybir.AluOpType

P = 128
PACK = 4
GRAD_SCALE = 0.04
MOM_SCALE = 0.9
FUSED = 256
PIECE = 128


def tile_list_wgrad_lists_on_both_sides_kernel(tc, xt, gj, mom, offs, offs2, out):
    nc = tc.nc
    xt_rows = xt.rearrange("(p t) n -> p t n", t=PACK)
    gj_rows = gj.rearrange("(p t) n -> p t n", t=PACK)
    mom_rows = mom.rearrange("(p t) n -> p t n", t=PACK)
    out_rows = out.rearrange("(p t) n -> p t n", t=PACK)

    with ExitStack() as ctx:
        keep = ctx.enter_context(tc.tile_pool(name="keep", bufs=1))
        stage = ctx.enter_context(tc.tile_pool(name="stage", bufs=2))
        psum = ctx.enter_context(tc.psum_pool(name="psum", bufs=2))
        banks = ctx.enter_context(tc.psum_pool(name="banks", bufs=1))

        tok = keep.tile([P, J // 16], U16, name="tok")
        feat = keep.tile([P, I // 16], U16, name="feat")
        x_win = [keep.tile([P, T], F32, name="x_win%d" % t) for t in range(PACK)]
        g_win = [keep.tile([P, N], F32, name="g_win%d" % t) for t in range(PACK)]
        m_win = [keep.tile([P, N], F32, name="m_win%d" % t) for t in range(PACK)]

        nc.sync.dma_start(g_win[0][:], gj_rows[:, 0, :])
        nc.sync.dma_start(feat[:], offs2)
        nc.sync.dma_start(tok[:], offs)
        for t in range(1, PACK):
            nc.sync.dma_start(g_win[t][:], gj_rows[:, t, :])
        for t in range(PACK):
            nc.sync.dma_start(x_win[t][:], xt_rows[:, t, :])
        for t in range(PACK):
            nc.sync.dma_start(m_win[t][:], mom_rows[:, t, :])

        ident = keep.tile([P, P], F32, name="ident")
        make_identity(nc, ident[:])

        g_picked = keep.tile([P, PACK, I], BF16, name="g_picked")
        for t in range(PACK):
            nc.scalar.activation(g_picked[:, t, :], g_win[t][:].indirect(feat[:]), ACT.Copy)
        g_grouped = keep.tile([P, I, PACK], BF16, name="g_grouped", align_bytes=64)
        nc.vector.tensor_copy(
            g_grouped[:].rearrange("p (c i) t -> p c t i", i=4),
            g_picked[:].rearrange("p t (c i) -> p c t i", i=4),
        )
        g_codes = keep.tile([P, I], U32, name="g_codes", align_bytes=64)
        g_scales = keep.tile([P, I], U8, name="g_scales", align_bytes=64)
        nc.vector.quantize_mx(
            out=g_codes[:].bitcast(E5M2X4),
            scales=g_scales[:],
            in_=g_grouped[:].rearrange("p i t -> p (i t)"),
        )

        fused = slice(0, FUSED)
        plain = slice(FUSED, I)
        sums = []
        w_scaled = []
        for t in range(PACK):
            x_picked = stage.tile([P, J], BF16, name="x_picked")
            nc.scalar.activation(x_picked[:], x_win[t][:].indirect(tok[:]), ACT.Copy)
            words = x_picked[:].bitcast(F32)
            turned = psum.tile([P, 2, P], F32, name="turned")
            for u in range(2):
                nc.tensor.transpose(turned[:, u, :], words[:, u : J // 2 : 2], ident[:])
            x_grouped = stage.tile([P, P * PACK], BF16, name="x_grouped", align_bytes=64)
            nc.vector.tensor_copy(
                x_grouped[:].bitcast(F32).rearrange("p (r u) -> p r u", u=2),
                turned[:].rearrange("p u r -> p r u"),
            )
            x_codes = stage.tile([P, P], U32, name="x_codes", align_bytes=64)
            x_scales = stage.tile([P, P], U8, name="x_scales", align_bytes=64)
            nc.vector.quantize_mx(out=x_codes[:].bitcast(E4M3X4), scales=x_scales[:], in_=x_grouped[:])
            w = banks.tile([P, I], F32, name="w%d" % t)
            nc.tensor.matmul_mx(
                out=w[:],
                lhsT=x_codes[:].bitcast(E4M3X4),
                lhsT_scale=x_scales[:],
                rhs=g_codes[:].bitcast(E5M2X4),
                rhs_scale=g_scales[:],
                start=True,
                stop=True,
            )
            sums.append(w)
            scaled = stage.tile([P, FUSED], F32, name="scaled")
            nc.vector.tensor_scalar(scaled[:], w[:, fused], GRAD_SCALE / MOM_SCALE, None, ALU.mult)
            w_scaled.append(scaled)

        for t in range(PACK):
            result = keep.tile([P, I], F32, name="result%d" % t)
            mixed = stage.tile([P, I], F32, name="mixed")
            picked = stage.tile([P, I - FUSED], F32, name="picked")
            for c in range(0, FUSED, PIECE):
                nc.vector.tensor_tensor(
                    mixed[:, c : c + PIECE],
                    m_win[t][:].indirect(feat[:, c // 16 : (c + PIECE) // 16]),
                    w_scaled[t][:, c : c + PIECE],
                    ALU.add,
                )
            for c in range(FUSED, I, PIECE):
                nc.scalar.activation(
                    picked[:, c - FUSED : c - FUSED + PIECE],
                    m_win[t][:].indirect(feat[:, c // 16 : (c + PIECE) // 16]),
                    ACT.Copy,
                )
            for c in range(FUSED, I, PIECE):
                nc.vector.scalar_tensor_tensor(
                    mixed[:, c : c + PIECE],
                    sums[t][:, c : c + PIECE],
                    GRAD_SCALE / MOM_SCALE,
                    picked[:, c - FUSED : c - FUSED + PIECE],
                    ALU.mult,
                    ALU.add,
                )
            for c in range(0, I, PIECE):
                nc.scalar.activation(result[:, c : c + PIECE], mixed[:, c : c + PIECE], ACT.Tanh, scale=MOM_SCALE)
            if t < PACK - 1:
                nc.sync.dma_start(out_rows[:, t, :], result[:])
            else:
                nc.sync.dma_start(out_rows[:, t, fused], result[:, fused])
                nc.scalar.dma_start(out_rows[:, t, plain], result[:, plain])
